import numpy as np
import ml_dtypes


def mxq(x, axis, fmt="e4m3"):
    dtype, down = {"e4m3": (ml_dtypes.float8_e4m3fn, 7), "e5m2": (ml_dtypes.float8_e5m2, 14)}[fmt]
    v = np.moveaxis(np.asarray(x, np.float32).astype(ml_dtypes.bfloat16).astype(np.float64), axis, -1)
    blocks = v.reshape(v.shape[:-1] + (-1, 32))
    amax = np.abs(blocks).max(-1, keepdims=True)
    byte = np.maximum(np.where(amax > 0, np.frexp(amax)[1] - 1 + 127, 0) - down, 1)
    scale = np.exp2(byte - 127.0)
    codes = (blocks / scale).astype(np.float32).astype(dtype).astype(np.float64)
    return np.moveaxis((codes * scale).reshape(v.shape), -1, axis)


WIDE = False


def mx_kscale(k):
    if not WIDE:
        return np.ones(k)
    levels = np.array([10, -10, 5, -5, 0])
    if k % 512:
        return np.exp2(np.random.permutation(np.resize(levels, k // 32))).repeat(32)
    a = np.empty((k // 512, 16))
    for p in range(k // 512):
        a[p, :8] = np.random.permutation(np.resize(levels, 8))
        for g in range(8):
            far = levels[np.abs(levels - a[p, g]) >= 10]
            a[p, g + 8] = far[np.random.randint(len(far))]
    return np.exp2(a.ravel()).repeat(32)


BF16 = ml_dtypes.bfloat16


def bf(x):
    return np.asarray(x, np.float32).astype(BF16)


def f64(x):
    return np.asarray(x).astype(np.float64)


B, N, M, D, E = 2, 1024, 1024, 512, 512


def scaled_correlation(faq, fbq):
    depth = faq.shape[-1]
    return (faq @ fbq.transpose(0, 2, 1)) / np.sqrt(depth)


def mutual_filter(c):
    ra = np.max(c, axis=2, keepdims=True)
    rb = np.max(c, axis=1, keepdims=True)
    return c * (c / ra) * (c / rb)


def draw0():
    s = mx_kscale(D)
    t = mx_kscale(M)
    return {
        "fa": bf(np.random.standard_normal((B, N, D)) * s),
        "fb": bf(np.random.standard_normal((B, M, D)) / s),
        "g": bf((1.0 + 0.1 * np.random.standard_normal(M)) * t),
        "wt": bf(2.0 * np.random.standard_normal((M, E)) / np.sqrt(M) / t[:, None]),
        "wr": bf(0.5 * np.random.standard_normal((D, E)) / np.sqrt(D) / s[:, None]),
    }


def core(fa, fb, g, wt, wr):
    faq = mxq(f64(fa), 2, "e4m3")
    c = scaled_correlation(faq, mxq(f64(fb), 2, "e4m3"))
    f = mutual_filter(c)
    fg = f * f64(g)[None, None, :]
    t = mxq(fg, 2, "e4m3") @ mxq(f64(wt), 0, "e4m3")
    r = faq @ mxq(f64(wr), 0, "e4m3")
    return t + r


def e4m3fn_bytes(y):
    return np.clip(np.asarray(y, np.float64), -448.0, 448.0).astype(np.float32).astype(ml_dtypes.float8_e4m3fn).view(np.uint8)


def e4m3fn_values(b):
    return np.asarray(b, np.uint8).view(ml_dtypes.float8_e4m3fn).astype(np.float64)


def setup_inputs():
    d = draw0()
    x0 = np.asarray(d['fb']).astype(np.float64)
    s = (np.max(np.abs(x0), axis=(0, 1), keepdims=True) / 448.0).astype(np.float32)
    out = {}
    for k, v in d.items():
        if k == 'fb':
            out['fb_bytes'] = e4m3fn_bytes(x0 / s.astype(np.float64))
            out['fb_scale'] = s
        else:
            out[k] = v
    return out


def reference(fa, fb_bytes, fb_scale, g, wt, wr):
    return core(fa, e4m3fn_values(fb_bytes) * fb_scale.astype(np.float64), g, wt, wr)

@@ -1,0 +1,392 @@
+from contextlib import ExitStack
+
+import concourse.mybir as mybir
+from concourse.masks import make_identity
+
+F32 = mybir.dt.float32
+BF16 = mybir.dt.bfloat16
+U32 = mybir.dt.uint32
+U8 = mybir.dt.uint8
+FP8 = mybir.dt.float8_e4m3fn
+FP8X4 = mybir.dt.float8_e4m3fn_x4
+ALU = mybir.AluOpType
+ACT = mybir.ActivationFunctionType
+X = mybir.AxisListType.X
+
+B, N, M, D, E = 2, 1024, 1024, 512, 512
+P = 128
+NT = N // P
+FLOPS = 2 * B * N * M * D + 2 * B * N * M * E + 2 * B * N * D * E
+
+TURN_A = [1, 3, 5, 7]
+QUANT_A = [3, 5, 7, 9]
+TURN_B = [9, 11, 13, 15]
+QUANT_B = [11, 13, 15, -1]
+T1 = [[0, 1], [2], [3], [4], [5], [6], [7]]
+S1_AT = [3, 6]
+
+
+def tile_mutualfiltercosttokenencoder_kernel(tc, fa, fb_bytes, fb_scale, g, wt, wr, out):
+    nc = tc.nc
+    with ExitStack() as ctx:
+        keep = ctx.enter_context(tc.tile_pool(name="keep", bufs=1))
+        work = ctx.enter_context(tc.tile_pool(name="work", bufs=3))
+        cps = ctx.enter_context(tc.psum_pool(name="cps", bufs=5))
+        xps = ctx.enter_context(tc.psum_pool(name="xps", bufs=3))
+
+        def kt(shape, dt, nm):
+            return keep.tile(shape, dt, name=nm, tag=nm, align_bytes=64)
+
+        def wk(shape, dt, nm, bufs=3):
+            return work.tile(shape, dt, name=nm, tag=nm, bufs=bufs, align_bytes=64)
+
+        def cbank():
+            return cps.tile([P, 512], F32, name="cbank", tag="c")
+
+        def xbank():
+            return xps.tile([P, 512], F32, name="xbank", tag="x")
+
+        ident = kt([P, P], F32, "ident")
+        sc4 = kt([P, 4], F32, "sc4")
+        scb = kt([P, 512], F32, "scb")
+        graw = kt([P, 256], BF16, "graw")
+        gperm = kt([P, 2, 128], F32, "gperm")
+        gcol = kt([P, NT], F32, "gcol")
+        dummy = kt([P, 1], F32, "dummy")
+        fb_raw = [kt([P, 8, 512], U8, f"fb_raw{b}") for b in range(B)]
+        fb_w = [kt([P, 8, 512], BF16, f"fb_w{b}") for b in range(B)]
+        fa_raw = [kt([P, 8, 512], BF16, f"fa_raw{b}") for b in range(B)]
+        fa_q = [kt([P, N], U32, f"fa_q{b}") for b in range(B)]
+        fa_s = [kt([P, N], U8, f"fa_s{b}") for b in range(B)]
+        fb_q = [kt([P, M], U32, f"fb_q{b}") for b in range(B)]
+        fb_s = [kt([P, M], U8, f"fb_s{b}") for b in range(B)]
+        wt_raw = kt([P, 2, 4, E], BF16, "wt_raw")
+        wt_g = kt([P, 2, E, 4], BF16, "wt_g")
+        wt_q = kt([P, 2, E], U32, "wt_q")
+        wt_s = kt([P, 2, E], U8, "wt_s")
+        wr_raw = kt([P, 4, E], BF16, "wr_raw")
+        wr_g = kt([P, E, 4], BF16, "wr_g")
+        wr_q = kt([P, E], U32, "wr_q")
+        wr_s = kt([P, E], U8, "wr_s")
+        tmax = [kt([P, 2, NT], F32, f"tmax{b}") for b in range(B)]
+        srow = [kt([P, 3, NT], F32, f"srow{b}") for b in range(B)]
+        smap = [kt([P, M], F32, f"smap{b}") for b in range(B)]
+
+        ctx.enter_context(tc.manual_schedule())
+
+        fbv = [fb_bytes[b].rearrange("(g p j) d -> p g j d", g=2, j=4) for b in range(B)]
+        fav = [fa[b].rearrange("(p i) d -> p i d", i=8) for b in range(B)]
+
+        def load_fb(b, gg):
+            nc.sync.dma_start(out=fb_raw[b][:, 4 * gg : 4 * gg + 4, :], in_=fbv[b][:, gg])
+
+        def load_fa(b, i0, i1):
+            nc.sync.dma_start(out=fa_raw[b][:, i0:i1, :], in_=fav[b][:, i0:i1, :])
+
+        nc.sync.dma_start(out=sc4[:], in_=fb_scale.rearrange("o b (p j) -> p (o b j)", j=4))
+        load_fb(0, 0)
+        load_fb(0, 1)
+        for q in range(4):
+            load_fa(0, 2 * q, 2 * q + 2)
+        make_identity(nc, ident[:])
+        nc.gpsimd.memset(graw[:], 0.0)
+        nc.vector.memset(dummy[:], 0.0)
+        nc.scalar.activation(out=dummy[:], in_=dummy[:], func=ACT.Square)
+        load_fb(1, 0)
+        load_fb(1, 1)
+        load_fa(1, 0, 4)
+        load_fa(1, 4, 8)
+        nc.sync.dma_start(out=graw[0:4, :], in_=g.rearrange("(r f) -> r f", r=4))
+        nc.sync.dma_start(out=wr_raw[:], in_=wr.rearrange("(p t) e -> p t e", t=4))
+        nc.sync.dma_start(out=wt_raw[:], in_=wt.rearrange("(g p t) e -> p g t e", g=2, t=4))
+
+        scp = xbank()
+        for j in range(4):
+            nc.tensor.transpose(scp[:, 128 * j : 128 * j + 128], sc4[:, j : j + 1].to_broadcast([P, P]), ident[:])
+        nc.scalar.copy(out=scb[:].rearrange("q (p j) -> q p j", j=4), in_=scp[:].rearrange("q (j p) -> q p j", j=4))
+
+        def widen_v(b, gj):
+            nc.vector.tensor_tensor(out=fb_w[b][:, gj, :], in0=fb_raw[b][:, gj, :].bitcast(FP8), in1=scb[:], op=ALU.mult)
+
+        def widen_s(b, gj):
+            cast = wk([P, 512], BF16, "cast", bufs=4)
+            nc.scalar.copy(out=cast[:], in_=fb_raw[b][:, gj, :].bitcast(FP8))
+            return cast
+
+        def widen_g(b, gj, cast):
+            nc.gpsimd.tensor_tensor(out=fb_w[b][:, gj, :], in0=cast[:], in1=scb[:], op=ALU.mult)
+
+        def turn(b, which, q, bank):
+            src = fa_raw[b] if which == "a" else fb_w[b]
+            for r in range(2):
+                words = src[:, 2 * q + r, :].bitcast(F32)
+                for du in range(2):
+                    nc.tensor.transpose(bank[:, (2 * r + du) * 128 : (2 * r + du + 1) * 128], words[:, du::2], ident[:])
+
+        def turn_copy(which, bank):
+            grp = wk([P, 1024], BF16, "grp", bufs=6)
+            if which == "a":
+                nc.scalar.copy(
+                    out=grp[:].bitcast(F32).rearrange("d (i r u) -> d i r u", i=2, u=2),
+                    in_=bank[:].rearrange("d (i u r) -> d i r u", i=2, u=2),
+                )
+            else:
+                nc.scalar.copy(
+                    out=grp[:].bitcast(F32).rearrange("d (r e u) -> d r e u", e=2, u=2),
+                    in_=bank[:].rearrange("d (e u r) -> d r e u", e=2, u=2),
+                )
+            return grp
+
+        def turn_quant(b, which, q, grp):
+            dst, sca = (fa_q[b], fa_s[b]) if which == "a" else (fb_q[b], fb_s[b])
+            cols = slice(256 * q, 256 * q + 256)
+            nc.vector.quantize_mx(out=dst[:, cols].bitcast(FP8X4), scales=sca[:, cols], in_=grp[:])
+
+        grps = {}
+
+        def do_turn(b, which, q, bank):
+            turn(b, which, q, bank)
+            grps[(b, which, q)] = turn_copy(which, bank)
+
+        def do_quant(b, which, q):
+            turn_quant(b, which, q, grps[(b, which, q)])
+
+        def make_gcol():
+            gps = xbank()
+            for u in range(2):
+                nc.tensor.transpose(gps[:, 128 * u : 128 * u + 128], gperm[:, u, :], ident[:])
+            for u in range(2):
+                nc.vector.tensor_scalar(
+                    out=gcol[:].rearrange("q (g u h) -> q u g h", g=2, u=2)[:, u],
+                    in0=gps[:, 128 * u : 128 * u + 4].rearrange("q (g h) -> q g h", g=2),
+                    scalar1=float(D) ** -0.5, scalar2=None, op0=ALU.mult,
+                )
+
+        def mm_c(b, lq, ls, rq, rs, i, h, bank):
+            nc.tensor.matmul_mx(
+                out=bank[:],
+                lhsT=lq[b][:, 128 * i : 128 * i + 128].bitcast(FP8X4),
+                lhsT_scale=ls[b][:, 128 * i : 128 * i + 128],
+                rhs=rq[b][:, 512 * h : 512 * h + 512].bitcast(FP8X4),
+                rhs_scale=rs[b][:, 512 * h : 512 * h + 512],
+                start=True, stop=True,
+            )
+
+        def mm_t(b, i, h, bank):
+            mm_c(b, fb_q, fb_s, fa_q, fa_s, i, h, bank)
+
+        def mm_n(b, i, h, bank):
+            mm_c(b, fa_q, fa_s, fb_q, fb_s, i, h, bank)
+
+        def rd_t(b, i, h, bank):
+            nc.vector.reduce_max(out=tmax[b][:, h, i : i + 1], in_=bank[:], axis=X)
+
+        def s_cols(b, half, step):
+            cols = slice(4 * half, 4 * half + 4)
+            if step == 0:
+                nc.vector.tensor_tensor(out=srow[b][:, 0, cols], in0=tmax[b][:, 0, cols], in1=tmax[b][:, 1, cols], op=ALU.max)
+            elif step == 1:
+                nc.vector.reciprocal(out=srow[b][:, 1, cols], in_=srow[b][:, 0, cols])
+            else:
+                nc.vector.tensor_tensor(out=srow[b][:, 2, cols], in0=srow[b][:, 1, cols], in1=gcol[:, cols], op=ALU.mult)
+
+        def s_map(b, half):
+            bank = xbank()
+            for k in range(4):
+                i = 4 * half + k
+                nc.tensor.transpose(bank[:, 128 * k : 128 * k + 128], srow[b][:, 2, i : i + 1].to_broadcast([P, P]), ident[:])
+            nc.scalar.copy(out=smap[b][:, 512 * half : 512 * half + 512], in_=bank[:])
+
+
+        cast6 = widen_s(0, 6)
+        cast7 = widen_s(0, 7)
+        widen_g(0, 6, cast6)
+        widen_g(0, 7, cast7)
+        nc.gpsimd.tensor_copy(
+            out=gperm[:].rearrange("r u (q e) -> r u q e", e=2),
+            in_=graw[:].rearrange("r (q u e) -> r u q e", u=2, e=2),
+        )
+        widen_v(0, 0)
+        widen_v(0, 1)
+        do_turn(0, "a", 0, cbank())
+        do_turn(0, "b", 0, cbank())
+        widen_v(0, 2)
+        widen_v(0, 3)
+        do_turn(0, "a", 1, cbank())
+        do_turn(0, "a", 2, cbank())
+        do_turn(0, "a", 3, cbank())
+        widen_v(0, 4)
+        do_quant(0, "a", 0)
+        widen_v(0, 5)
+        do_quant(0, "b", 0)
+        do_turn(0, "b", 1, xbank())
+        do_quant(0, "a", 1)
+        do_quant(0, "a", 2)
+        do_quant(0, "a", 3)
+
+        order = [(i, h) for i in range(NT) for h in range(2)]
+        tb = {}
+
+        def issue_t0(k):
+            if k < 16:
+                tb[k] = cbank()
+                mm_t(0, order[k][0], order[k][1], tb[k])
+
+        for k in range(4):
+            issue_t0(k)
+        casts = {}
+        for i in range(NT):
+            if i == 0:
+                do_turn(0, "b", 2, xbank())
+            if i == 1:
+                do_turn(0, "b", 3, xbank())
+            for h in range(2):
+                k = 2 * i + h
+                if k < 8:
+                    casts[k] = widen_s(1, k)
+                    widen_g(1, k, casts[k])
+                rd_t(0, i, h, tb[k])
+                if k == 0:
+                    do_quant(0, "b", 1)
+                if k == 3:
+                    do_quant(0, "b", 2)
+                if k == 6:
+                    do_quant(0, "b", 3)
+                if k == 4:
+                    make_gcol()
+                if k in TURN_A:
+                    do_turn(1, "a", TURN_A.index(k), xbank())
+                if k in QUANT_A:
+                    do_quant(1, "a", QUANT_A.index(k))
+                if k in TURN_B:
+                    do_turn(1, "b", TURN_B.index(k), xbank())
+                if k in QUANT_B:
+                    do_quant(1, "b", QUANT_B.index(k))
+                if k in (8, 10, 12):
+                    s_cols(0, 0, (k - 8) // 2)
+                if k == 13:
+                    s_map(0, 0)
+                issue_t0(k + 4)
+        for t in range(2):
+            nc.gpsimd.tensor_scalar(
+                out=wt_g[:, t], in0=wt_raw[:, t].rearrange("p t e -> p e t"),
+                scalar1=1.0, scalar2=1.0, op0=ALU.mult, op1=ALU.mult,
+            )
+        nc.scalar.copy(out=wr_g[:], in_=wr_raw[:].rearrange("p t e -> p e t"))
+
+        STEPS = 2 * NT
+        nb, sq, fgt, amx, arc, grpf = {}, {}, {}, {}, {}, {}
+
+        def issue_n(s, h):
+            if s < STEPS:
+                nb[(s, h)] = cbank()
+                mm_n(s // NT, s % NT, h, nb[(s, h)])
+
+        issue_n(0, 0)
+        issue_n(0, 1)
+        t1 = [list(x) for x in T1]
+        t1_done = 0
+        do_quant(1, "b", 3)
+
+        for s in range(STEPS + 3):
+            b, i = s // NT, s % NT
+            p1, p2 = s - 1, s - 2
+            live = s < STEPS
+            tq = [(it, h) for it in (t1[s] if s < len(t1) else []) for h in range(2)]
+            tbk = []
+
+            def t_mm():
+                if len(tbk) < len(tq):
+                    bank = xbank()
+                    mm_t(1, tq[len(tbk)][0], tq[len(tbk)][1], bank)
+                    tbk.append(bank)
+
+            tdone = [0]
+
+            def t_rd():
+                k = tdone[0]
+                if k < len(tbk):
+                    rd_t(1, tq[k][0], tq[k][1], tbk[k])
+                    tdone[0] = k + 1
+
+            t_mm()
+            if live:
+                amx[s] = wk([P, 2], F32, "amx", bufs=4)
+                arc[s] = wk([P, 2], F32, "arc", bufs=4)
+                sq[s] = wk([P, M], F32, "sq", bufs=4)
+                nc.vector.reduce_max(out=amx[s][:, 0:1], in_=nb[(s, 0)][:], axis=X)
+            if s == 0:
+                s_cols(0, 1, 0)
+            if 0 <= p2 < STEPS:
+                words = fgt[p2][:].bitcast(F32)
+                bank = xbank()
+                for k in range(4):
+                    nc.tensor.transpose(bank[:, 128 * k : 128 * k + 128], words[:, 128 * k : 128 * k + 128], ident[:])
+                grpf[p2] = wk([P, 1024], BF16, "grpf")
+                nc.scalar.copy(
+                    out=grpf[p2][:].bitcast(F32).rearrange("p (g n u) -> p g n u", g=2, u=2),
+                    in_=bank[:].rearrange("p (g u n) -> p g n u", g=2, u=2),
+                )
+            t_mm()
+            if live:
+                nc.vector.reduce_max(out=amx[s][:, 1:2], in_=nb[(s, 1)][:], axis=X)
+                if s == 0:
+                    s_cols(0, 1, 1)
+                for h in range(2):
+                    cols = slice(512 * h, 512 * h + 512)
+                    nc.scalar.activation(out=sq[s][:, cols], in_=nb[(s, h)][:], func=ACT.Square)
+                    if not (s == 0 and h == 1):
+                        nc.gpsimd.tensor_tensor(out=sq[s][:, cols], in0=sq[s][:, cols], in1=smap[b][:, cols], op=ALU.mult)
+            t_rd()
+            if s == 0:
+                s_cols(0, 1, 2)
+                s_map(0, 1)
+                nc.gpsimd.tensor_tensor(out=sq[0][:, 512:], in0=sq[0][:, 512:], in1=smap[0][:, 512:], op=ALU.mult)
+            if 0 <= p2 < STEPS:
+                b2, i2 = p2 // NT, p2 % NT
+                fq = wk([P, 256], U32, "fq")
+                fs = wk([P, 256], U8, "fs")
+                nc.vector.quantize_mx(out=fq[:].bitcast(FP8X4), scales=fs[:], in_=grpf[p2][:])
+                o = xbank()
+                rows = slice(128 * i2, 128 * i2 + 128)
+                nc.tensor.matmul_mx(
+                    out=o[:], lhsT=fa_q[b2][:, rows].bitcast(FP8X4), lhsT_scale=fa_s[b2][:, rows],
+                    rhs=wr_q[:].bitcast(FP8X4), rhs_scale=wr_s[:], start=True, stop=False,
+                )
+                for t in range(2):
+                    nc.tensor.matmul_mx(
+                        out=o[:], lhsT=fq[:, 128 * t : 128 * t + 128].bitcast(FP8X4), lhsT_scale=fs[:, 128 * t : 128 * t + 128],
+                        rhs=wt_q[:, t].bitcast(FP8X4), rhs_scale=wt_s[:, t], start=False, stop=(t == 1),
+                    )
+                ot = wk([P, E], F32, "ot", bufs=4)
+                nc.scalar.copy(out=ot[:], in_=o[:])
+                nc.sync.dma_start(out=out[b2].rearrange("(p i) e -> p i e", i=8)[:, i2, :], in_=ot[:])
+            if 0 <= p1 < STEPS:
+                fgt[p1] = wk([P, M], BF16, "fg")
+            for h in range(2):
+                if 0 <= p1 < STEPS:
+                    cols = slice(512 * h, 512 * h + 512)
+                    nc.vector.scalar_tensor_tensor(
+                        out=fgt[p1][:, cols], in0=nb[(p1, h)][:], scalar=arc[p1][:, 1:2], in1=sq[p1][:, cols],
+                        op0=ALU.mult, op1=ALU.mult,
+                    )
+                if live and h == 0:
+                    nc.vector.tensor_tensor(out=arc[s][:, 0:1], in0=amx[s][:, 0:1], in1=amx[s][:, 1:2], op=ALU.max)
+                t_rd()
+                issue_n(s + 1, h)
+            if live:
+                nc.vector.reciprocal(out=arc[s][:, 1:2], in_=arc[s][:, 0:1])
+            while tdone[0] < len(tq):
+                t_mm()
+                t_rd()
+            if s == 0:
+                for t in range(2):
+                    nc.vector.quantize_mx(
+                        out=wt_q[:, t].bitcast(FP8X4), scales=wt_s[:, t], in_=wt_g[:, t].rearrange("p e t -> p (e t)")
+                    )
+                nc.vector.quantize_mx(out=wr_q[:].bitcast(FP8X4), scales=wr_s[:], in_=wr_g[:].rearrange("p e t -> p (e t)"))
+            if s in S1_AT:
+                half = S1_AT.index(s)
+                for step in range(3):
+                    s_cols(1, half, step)
+                s_map(1, half)

@@ -18,12 +18,26 @@ P = 128
 NT = N // P
 FLOPS = 2 * B * N * M * D + 2 * B * N * M * E + 2 * B * N * D * E
 
-TURN_A = [1, 3, 5, 7]
-QUANT_A = [3, 5, 7, 9]
-TURN_B = [9, 11, 13, 15]
-QUANT_B = [11, 13, 15, -1]
-T1 = [[0, 1], [2], [3], [4], [5], [6], [7]]
-S1_AT = [3, 6]
+HEAD = [("W", 0, 0), ("W", 0, 1), ("U", 0, "a", 0), ("W", 0, 2), ("W", 0, 3), ("U", 0, "b", 0), ("U", 0, "a", 1), ("W", 0, 4), ("W", 0, 5), ("U", 0, "a", 2), ("T", 0, "b", 1), ("Q", 0, "a", 0), ("W", 0, 6), ("W", 0, 7), ("U", 0, "a", 3), ("T", 0, "b", 2),
+ ("Q", 0, "b", 0), ("W", 1, 0), ("T", 0, "b", 3), ("Q", 0, "a", 1), ("W", 1, 1), ("Q", 0, "a", 2), ("Q", 0, "b", 1), ("W", 1, 2), ("Q", 0, "a", 3), ("Q", 0, "b", 2), ("W", 1, 3), ("Q", 0, "b", 3)]
+PLAN = {
+    0: [("G",), ("T", 1, "a", 0)],
+    1: [("C", 4), ("T", 1, "a", 1)],
+    2: [("C", 5)],
+    3: [("C", 6), ("T", 1, "a", 2)],
+    4: [("C", 7)],
+    5: [("T", 1, "a", 3), ("I", 0)],
+    7: [("T", 1, "b", 0)],
+    9: [("S", 0, 0, 0), ("T", 1, "b", 1)],
+    10: [("S", 0, 0, 1)],
+    11: [("T", 1, "b", 2)],
+    13: [("T", 1, "b", 3)],
+    15: [("Q", 1, "a", 0), ("S", 0, 0, 2), ("S", 0, 1, 0), ("Q", 1, "a", 1), ("S", 0, 1, 1), ("M", 0, 0), ("Q", 1, "a", 2), ("S", 0, 1, 2), ("Q", 1, "a", 3), ("M", 0, 1),
+         ("K", 0), ("Q", 1, "b", 0), ("Q", 1, "b", 1), ("Q", 1, "b", 2), ("Q", 1, "b", 3)],
+}
+MAIN = {(0, 1): [("J", 0), ("J", 1)], (0, 2): [("J", 2), ("J", 3)], (0, 3): [("H", 0), ("H", 1)], (1, 1): [("L",), ("H", 2)], (1, 2): [("H", 3)], (2, 1): [("K", 1)],
+    (3, 3): [("S", 1, 0, 0)], (4, 0): [("S", 1, 0, 1), ("S", 1, 0, 2)], (4, 3): [("M", 1, 0)], (5, 3): [("S", 1, 1, 0)], (6, 0): [("S", 1, 1, 1), ("S", 1, 1, 2)], (7, 0): [("M", 1, 1)]}
+T1 = [[0, 1], [2], [3], [4], [5], [6, 7]]
 
 
 def tile_mutualfiltercosttokenencoder_kernel(tc, fa, fb_bytes, fb_scale, g, wt, wr, out):
@@ -77,6 +91,8 @@ def tile_mutualfiltercosttokenencoder_kernel(tc, fa, fb_bytes, fb_scale, g, wt, 
         fbv = [fb_bytes[b].rearrange("(g p j) d -> p g j d", g=2, j=4) for b in range(B)]
         fav = [fa[b].rearrange("(p i) d -> p i d", i=8) for b in range(B)]
 
+        nc.gpsimd.memset(graw[:], 0.0)
+
         def load_fb(b, gg):
             nc.sync.dma_start(out=fb_raw[b][:, 4 * gg : 4 * gg + 4, :], in_=fbv[b][:, gg])
 
@@ -86,17 +102,16 @@ def tile_mutualfiltercosttokenencoder_kernel(tc, fa, fb_bytes, fb_scale, g, wt, 
         nc.sync.dma_start(out=sc4[:], in_=fb_scale.rearrange("o b (p j) -> p (o b j)", j=4))
         load_fb(0, 0)
         load_fb(0, 1)
+        nc.sync.dma_start(out=graw[0:4, :], in_=g.rearrange("(r f) -> r f", r=4))
         for q in range(4):
             load_fa(0, 2 * q, 2 * q + 2)
         make_identity(nc, ident[:])
-        nc.gpsimd.memset(graw[:], 0.0)
         nc.vector.memset(dummy[:], 0.0)
         nc.scalar.activation(out=dummy[:], in_=dummy[:], func=ACT.Square)
         load_fb(1, 0)
         load_fb(1, 1)
         load_fa(1, 0, 4)
         load_fa(1, 4, 8)
-        nc.sync.dma_start(out=graw[0:4, :], in_=g.rearrange("(r f) -> r f", r=4))
         nc.sync.dma_start(out=wr_raw[:], in_=wr.rearrange("(p t) e -> p t e", t=4))
         nc.sync.dma_start(out=wt_raw[:], in_=wt.rearrange("(g p t) e -> p g t e", g=2, t=4))
 
@@ -124,7 +139,7 @@ def tile_mutualfiltercosttokenencoder_kernel(tc, fa, fb_bytes, fb_scale, g, wt, 
                     nc.tensor.transpose(bank[:, (2 * r + du) * 128 : (2 * r + du + 1) * 128], words[:, du::2], ident[:])
 
         def turn_copy(which, bank):
-            grp = wk([P, 1024], BF16, "grp", bufs=6)
+            grp = wk([P, 1024], BF16, "grp", bufs=8)
             if which == "a":
                 nc.scalar.copy(
                     out=grp[:].bitcast(F32).rearrange("d (i r u) -> d i r u", i=2, u=2),
@@ -184,11 +199,12 @@ def tile_mutualfiltercosttokenencoder_kernel(tc, fa, fb_bytes, fb_scale, g, wt, 
         def s_cols(b, half, step):
             cols = slice(4 * half, 4 * half + 4)
             if step == 0:
-                nc.vector.tensor_tensor(out=srow[b][:, 0, cols], in0=tmax[b][:, 0, cols], in1=tmax[b][:, 1, cols], op=ALU.max)
+                nc.vector.reduce_max(out=srow[b][:, 0, cols], in_=tmax[b][:, :, cols].rearrange("q h i -> q i h"), axis=X)
             elif step == 1:
                 nc.vector.reciprocal(out=srow[b][:, 1, cols], in_=srow[b][:, 0, cols])
             else:
-                nc.vector.tensor_tensor(out=srow[b][:, 2, cols], in0=srow[b][:, 1, cols], in1=gcol[:, cols], op=ALU.mult)
+                eng = nc.vector if b == 0 else nc.gpsimd
+                eng.tensor_tensor(out=srow[b][:, 2, cols], in0=srow[b][:, 1, cols], in1=gcol[:, cols], op=ALU.mult)
 
         def s_map(b, half):
             bank = xbank()
@@ -198,81 +214,57 @@ def tile_mutualfiltercosttokenencoder_kernel(tc, fa, fb_bytes, fb_scale, g, wt, 
             nc.scalar.copy(out=smap[b][:, 512 * half : 512 * half + 512], in_=bank[:])
 
 
-        cast6 = widen_s(0, 6)
-        cast7 = widen_s(0, 7)
-        widen_g(0, 6, cast6)
-        widen_g(0, 7, cast7)
-        nc.gpsimd.tensor_copy(
-            out=gperm[:].rearrange("r u (q e) -> r u q e", e=2),
-            in_=graw[:].rearrange("r (q u e) -> r u q e", u=2, e=2),
+        nc.gpsimd.tensor_scalar(
+            out=gperm[:].rearrange("r u (q e) -> r u q e", e=2), in0=graw[:].rearrange("r (q u e) -> r u q e", u=2, e=2),
+            scalar1=1.0, scalar2=1.0, op0=ALU.mult, op1=ALU.mult,
         )
-        widen_v(0, 0)
-        widen_v(0, 1)
-        do_turn(0, "a", 0, cbank())
-        do_turn(0, "b", 0, cbank())
-        widen_v(0, 2)
-        widen_v(0, 3)
-        do_turn(0, "a", 1, cbank())
-        do_turn(0, "a", 2, cbank())
-        do_turn(0, "a", 3, cbank())
-        widen_v(0, 4)
-        do_quant(0, "a", 0)
-        widen_v(0, 5)
-        do_quant(0, "b", 0)
-        do_turn(0, "b", 1, xbank())
-        do_quant(0, "a", 1)
-        do_quant(0, "a", 2)
-        do_quant(0, "a", 3)
-
         order = [(i, h) for i in range(NT) for h in range(2)]
         tb = {}
+        casts = {}
 
         def issue_t0(k):
             if k < 16:
                 tb[k] = cbank()
                 mm_t(0, order[k][0], order[k][1], tb[k])
 
-        for k in range(4):
-            issue_t0(k)
-        casts = {}
-        for i in range(NT):
-            if i == 0:
-                do_turn(0, "b", 2, xbank())
-            if i == 1:
-                do_turn(0, "b", 3, xbank())
-            for h in range(2):
-                k = 2 * i + h
-                if k < 8:
-                    casts[k] = widen_s(1, k)
-                    widen_g(1, k, casts[k])
-                rd_t(0, i, h, tb[k])
-                if k == 0:
-                    do_quant(0, "b", 1)
-                if k == 3:
-                    do_quant(0, "b", 2)
-                if k == 6:
-                    do_quant(0, "b", 3)
-                if k == 4:
-                    make_gcol()
-                if k in TURN_A:
-                    do_turn(1, "a", TURN_A.index(k), xbank())
-                if k in QUANT_A:
-                    do_quant(1, "a", QUANT_A.index(k))
-                if k in TURN_B:
-                    do_turn(1, "b", TURN_B.index(k), xbank())
-                if k in QUANT_B:
-                    do_quant(1, "b", QUANT_B.index(k))
-                if k in (8, 10, 12):
-                    s_cols(0, 0, (k - 8) // 2)
-                if k == 13:
-                    s_map(0, 0)
-                issue_t0(k + 4)
-        for t in range(2):
+        def cast_g(gj):
+            casts[gj] = widen_s(1, gj)
+            widen_g(1, gj, casts[gj])
+
+        def wt_i(t):
             nc.gpsimd.tensor_scalar(
                 out=wt_g[:, t], in0=wt_raw[:, t].rearrange("p t e -> p e t"),
                 scalar1=1.0, scalar2=1.0, op0=ALU.mult, op1=ALU.mult,
             )
-        nc.scalar.copy(out=wr_g[:], in_=wr_raw[:].rearrange("p t e -> p e t"))
+
+        def wt_quant(t):
+            nc.vector.quantize_mx(out=wt_q[:, t].bitcast(FP8X4), scales=wt_s[:, t], in_=wt_g[:, t].rearrange("p e t -> p (e t)"))
+
+        def wr_i(k):
+            cols = slice(128 * k, 128 * k + 128)
+            nc.scalar.copy(out=wr_g[:, cols], in_=wr_raw[:, :, cols].rearrange("p t e -> p e t"))
+
+        def wt_s_i(k):
+            cols = slice(128 * k, 128 * k + 128)
+            nc.scalar.copy(out=wt_g[:, 1, cols], in_=wt_raw[:, 1, :, cols].rearrange("p t e -> p e t"))
+
+        def wr_quant():
+            nc.vector.quantize_mx(out=wr_q[:].bitcast(FP8X4), scales=wr_s[:], in_=wr_g[:].rearrange("p e t -> p (e t)"))
+
+        ops = dict(
+            T=lambda b, w, q: do_turn(b, w, q, xbank()), U=lambda b, w, q: do_turn(b, w, q, cbank()), Q=do_quant, W=widen_v, C=cast_g, G=make_gcol,
+            S=s_cols, M=s_map, I=wt_i, J=wr_i, H=wt_s_i, K=wt_quant, L=wr_quant,
+        )
+        for o in HEAD:
+            ops[o[0]](*o[1:])
+
+        for k in range(4):
+            issue_t0(k)
+        for k in range(16):
+            rd_t(0, order[k][0], order[k][1], tb[k])
+            for o in PLAN.get(k, []):
+                ops[o[0]](*o[1:])
+            issue_t0(k + 4)
 
         STEPS = 2 * NT
         nb, sq, fgt, amx, arc, grpf = {}, {}, {}, {}, {}, {}
@@ -282,111 +274,128 @@ def tile_mutualfiltercosttokenencoder_kernel(tc, fa, fb_bytes, fb_scale, g, wt, 
                 nb[(s, h)] = cbank()
                 mm_n(s // NT, s % NT, h, nb[(s, h)])
 
+        def row_max(s, h):
+            nc.vector.reduce_max(out=amx[s][:, h : h + 1], in_=nb[(s, h)][:], axis=X)
+
+        def square(s, h):
+            cols = slice(512 * h, 512 * h + 512)
+            nc.scalar.activation(out=sq[s][:, cols], in_=nb[(s, h)][:], func=ACT.Square)
+
+        def weigh(s, h):
+            cols = slice(512 * h, 512 * h + 512)
+            nc.gpsimd.tensor_tensor(out=sq[s][:, cols], in0=sq[s][:, cols], in1=smap[s // NT][:, cols], op=ALU.mult)
+
+        def product(s, h):
+            cols = slice(512 * h, 512 * h + 512)
+            nc.vector.scalar_tensor_tensor(
+                out=fgt[s][:, cols], in0=nb[(s, h)][:], scalar=arc[s][:, 1:2], in1=sq[s][:, cols],
+                op0=ALU.mult, op1=ALU.mult,
+            )
+
+        fbk = {}
+
+        def turn_f(s, part):
+            if part == 0:
+                words = fgt[s][:].bitcast(F32)
+                fbk[s] = xbank()
+                for k in range(4):
+                    nc.tensor.transpose(fbk[s][:, 128 * k : 128 * k + 128], words[:, 128 * k : 128 * k + 128], ident[:])
+            else:
+                grpf[s] = wk([P, 1024], BF16, "grpf")
+                nc.scalar.copy(
+                    out=grpf[s][:].bitcast(F32).rearrange("p (g n u) -> p g n u", g=2, u=2),
+                    in_=fbk[s][:].rearrange("p (g u n) -> p g n u", g=2, u=2),
+                )
+
+        fqs = {}
+
+        def quant_f(s):
+            fq = wk([P, 256], U32, "fq")
+            fs = wk([P, 256], U8, "fs")
+            nc.vector.quantize_mx(out=fq[:].bitcast(FP8X4), scales=fs[:], in_=grpf[s][:])
+            fqs[s] = (fq, fs)
+
+        obs = {}
+
+        def mm_out(s):
+            b2, i2 = s // NT, s % NT
+            fq, fs = fqs[s]
+            o = xbank()
+            rows = slice(128 * i2, 128 * i2 + 128)
+            nc.tensor.matmul_mx(
+                out=o[:], lhsT=fa_q[b2][:, rows].bitcast(FP8X4), lhsT_scale=fa_s[b2][:, rows],
+                rhs=wr_q[:].bitcast(FP8X4), rhs_scale=wr_s[:], start=True, stop=False,
+            )
+            for t in range(2):
+                nc.tensor.matmul_mx(
+                    out=o[:], lhsT=fq[:, 128 * t : 128 * t + 128].bitcast(FP8X4), lhsT_scale=fs[:, 128 * t : 128 * t + 128],
+                    rhs=wt_q[:, t].bitcast(FP8X4), rhs_scale=wt_s[:, t], start=False, stop=(t == 1),
+                )
+            obs[s] = o
+
+        def store(s):
+            ot = wk([P, E], F32, "ot", bufs=4)
+            nc.scalar.copy(out=ot[:], in_=obs[s][:])
+            nc.sync.dma_start(out=out[s // NT].rearrange("(p i) e -> p i e", i=8)[:, s % NT, :], in_=ot[:])
+
         issue_n(0, 0)
         issue_n(0, 1)
-        t1 = [list(x) for x in T1]
-        t1_done = 0
-        do_quant(1, "b", 3)
-
         for s in range(STEPS + 3):
-            b, i = s // NT, s % NT
-            p1, p2 = s - 1, s - 2
-            live = s < STEPS
-            tq = [(it, h) for it in (t1[s] if s < len(t1) else []) for h in range(2)]
-            tbk = []
+            live, prv = s < STEPS, 1 <= s <= STEPS
+            tq = [(it, h) for it in (T1[s] if s < len(T1) else []) for h in range(2)]
+            tbk = {}
 
-            def t_mm():
-                if len(tbk) < len(tq):
-                    bank = xbank()
-                    mm_t(1, tq[len(tbk)][0], tq[len(tbk)][1], bank)
-                    tbk.append(bank)
+            def t_mm(k):
+                if k < len(tq):
+                    tbk[k] = xbank()
+                    mm_t(1, tq[k][0], tq[k][1], tbk[k])
 
-            tdone = [0]
-
-            def t_rd():
-                k = tdone[0]
-                if k < len(tbk):
+            def t_rd(k):
+                if k < len(tq):
                     rd_t(1, tq[k][0], tq[k][1], tbk[k])
-                    tdone[0] = k + 1
 
-            t_mm()
+            def extra(pos):
+                for o in MAIN.get((s, pos), []):
+                    ops[o[0]](*o[1:])
+
+            t_mm(0)
+            t_rd(0)
             if live:
                 amx[s] = wk([P, 2], F32, "amx", bufs=4)
                 arc[s] = wk([P, 2], F32, "arc", bufs=4)
                 sq[s] = wk([P, M], F32, "sq", bufs=4)
-                nc.vector.reduce_max(out=amx[s][:, 0:1], in_=nb[(s, 0)][:], axis=X)
-            if s == 0:
-                s_cols(0, 1, 0)
-            if 0 <= p2 < STEPS:
-                words = fgt[p2][:].bitcast(F32)
-                bank = xbank()
-                for k in range(4):
-                    nc.tensor.transpose(bank[:, 128 * k : 128 * k + 128], words[:, 128 * k : 128 * k + 128], ident[:])
-                grpf[p2] = wk([P, 1024], BF16, "grpf")
-                nc.scalar.copy(
-                    out=grpf[p2][:].bitcast(F32).rearrange("p (g n u) -> p g n u", g=2, u=2),
-                    in_=bank[:].rearrange("p (g u n) -> p g n u", g=2, u=2),
-                )
-            t_mm()
+                row_max(s, 0)
+                square(s, 0)
+                weigh(s, 0)
+            if 2 <= s <= STEPS + 1:
+                turn_f(s - 2, 0)
+            extra(0)
+            t_mm(1)
             if live:
-                nc.vector.reduce_max(out=amx[s][:, 1:2], in_=nb[(s, 1)][:], axis=X)
-                if s == 0:
-                    s_cols(0, 1, 1)
-                for h in range(2):
-                    cols = slice(512 * h, 512 * h + 512)
-                    nc.scalar.activation(out=sq[s][:, cols], in_=nb[(s, h)][:], func=ACT.Square)
-                    if not (s == 0 and h == 1):
-                        nc.gpsimd.tensor_tensor(out=sq[s][:, cols], in0=sq[s][:, cols], in1=smap[b][:, cols], op=ALU.mult)
-            t_rd()
-            if s == 0:
-                s_cols(0, 1, 2)
-                s_map(0, 1)
-                nc.gpsimd.tensor_tensor(out=sq[0][:, 512:], in0=sq[0][:, 512:], in1=smap[0][:, 512:], op=ALU.mult)
-            if 0 <= p2 < STEPS:
-                b2, i2 = p2 // NT, p2 % NT
-                fq = wk([P, 256], U32, "fq")
-                fs = wk([P, 256], U8, "fs")
-                nc.vector.quantize_mx(out=fq[:].bitcast(FP8X4), scales=fs[:], in_=grpf[p2][:])
-                o = xbank()
-                rows = slice(128 * i2, 128 * i2 + 128)
-                nc.tensor.matmul_mx(
-                    out=o[:], lhsT=fa_q[b2][:, rows].bitcast(FP8X4), lhsT_scale=fa_s[b2][:, rows],
-                    rhs=wr_q[:].bitcast(FP8X4), rhs_scale=wr_s[:], start=True, stop=False,
-                )
-                for t in range(2):
-                    nc.tensor.matmul_mx(
-                        out=o[:], lhsT=fq[:, 128 * t : 128 * t + 128].bitcast(FP8X4), lhsT_scale=fs[:, 128 * t : 128 * t + 128],
-                        rhs=wt_q[:, t].bitcast(FP8X4), rhs_scale=wt_s[:, t], start=False, stop=(t == 1),
-                    )
-                ot = wk([P, E], F32, "ot", bufs=4)
-                nc.scalar.copy(out=ot[:], in_=o[:])
-                nc.sync.dma_start(out=out[b2].rearrange("(p i) e -> p i e", i=8)[:, i2, :], in_=ot[:])
-            if 0 <= p1 < STEPS:
-                fgt[p1] = wk([P, M], BF16, "fg")
-            for h in range(2):
-                if 0 <= p1 < STEPS:
-                    cols = slice(512 * h, 512 * h + 512)
-                    nc.vector.scalar_tensor_tensor(
-                        out=fgt[p1][:, cols], in0=nb[(p1, h)][:], scalar=arc[p1][:, 1:2], in1=sq[p1][:, cols],
-                        op0=ALU.mult, op1=ALU.mult,
-                    )
-                if live and h == 0:
-                    nc.vector.tensor_tensor(out=arc[s][:, 0:1], in0=amx[s][:, 0:1], in1=amx[s][:, 1:2], op=ALU.max)
-                t_rd()
-                issue_n(s + 1, h)
+                row_max(s, 1)
+                square(s, 1)
+                weigh(s, 1)
+            if prv:
+                nc.vector.reciprocal(out=arc[s - 1][:, 1:2], in_=arc[s - 1][:, 0:1])
+                fgt[s - 1] = wk([P, M], BF16, "fg")
+            if 2 <= s <= STEPS + 1:
+                turn_f(s - 2, 1)
+            extra(1)
+            if s >= 3:
+                quant_f(s - 3)
+                mm_out(s - 3)
+                store(s - 3)
+            if prv:
+                product(s - 1, 0)
+            issue_n(s + 1, 0)
+            t_rd(1)
+            extra(2)
+            if prv:
+                product(s - 1, 1)
+            issue_n(s + 1, 1)
             if live:
-                nc.vector.reciprocal(out=arc[s][:, 1:2], in_=arc[s][:, 0:1])
-            while tdone[0] < len(tq):
-                t_mm()
-                t_rd()
-            if s == 0:
-                for t in range(2):
-                    nc.vector.quantize_mx(
-                        out=wt_q[:, t].bitcast(FP8X4), scales=wt_s[:, t], in_=wt_g[:, t].rearrange("p e t -> p (e t)")
-                    )
-                nc.vector.quantize_mx(out=wr_q[:].bitcast(FP8X4), scales=wr_s[:], in_=wr_g[:].rearrange("p e t -> p (e t)"))
-            if s in S1_AT:
-                half = S1_AT.index(s)
-                for step in range(3):
-                    s_cols(1, half, step)
-                s_map(1, half)
+                nc.vector.reduce_max(out=arc[s][:, 0:1], in_=amx[s][:], axis=X)
+            for k in range(2, len(tq)):
+                t_mm(k)
+                t_rd(k)
+            extra(3)

@@ -18,26 +18,11 @@ P = 128
 NT = N // P
 FLOPS = 2 * B * N * M * D + 2 * B * N * M * E + 2 * B * N * D * E
 
-HEAD = [("W", 0, 0), ("W", 0, 1), ("U", 0, "a", 0), ("W", 0, 2), ("W", 0, 3), ("U", 0, "b", 0), ("U", 0, "a", 1), ("W", 0, 4), ("W", 0, 5), ("U", 0, "a", 2), ("T", 0, "b", 1), ("Q", 0, "a", 0), ("W", 0, 6), ("W", 0, 7), ("U", 0, "a", 3), ("T", 0, "b", 2),
- ("Q", 0, "b", 0), ("W", 1, 0), ("T", 0, "b", 3), ("Q", 0, "a", 1), ("W", 1, 1), ("Q", 0, "a", 2), ("Q", 0, "b", 1), ("W", 1, 2), ("Q", 0, "a", 3), ("Q", 0, "b", 2), ("W", 1, 3), ("Q", 0, "b", 3)]
-PLAN = {
-    0: [("G",), ("T", 1, "a", 0)],
-    1: [("C", 4), ("T", 1, "a", 1)],
-    2: [("C", 5)],
-    3: [("C", 6), ("T", 1, "a", 2)],
-    4: [("C", 7)],
-    5: [("T", 1, "a", 3), ("I", 0)],
-    7: [("T", 1, "b", 0)],
-    9: [("S", 0, 0, 0), ("T", 1, "b", 1)],
-    10: [("S", 0, 0, 1)],
-    11: [("T", 1, "b", 2)],
-    13: [("T", 1, "b", 3)],
-    15: [("Q", 1, "a", 0), ("S", 0, 0, 2), ("S", 0, 1, 0), ("Q", 1, "a", 1), ("S", 0, 1, 1), ("M", 0, 0), ("Q", 1, "a", 2), ("S", 0, 1, 2), ("Q", 1, "a", 3), ("M", 0, 1),
-         ("K", 0), ("Q", 1, "b", 0), ("Q", 1, "b", 1), ("Q", 1, "b", 2), ("Q", 1, "b", 3)],
-}
-MAIN = {(0, 1): [("J", 0), ("J", 1)], (0, 2): [("J", 2), ("J", 3)], (0, 3): [("H", 0), ("H", 1)], (1, 1): [("L",), ("H", 2)], (1, 2): [("H", 3)], (2, 1): [("K", 1)],
-    (3, 3): [("S", 1, 0, 0)], (4, 0): [("S", 1, 0, 1), ("S", 1, 0, 2)], (4, 3): [("M", 1, 0)], (5, 3): [("S", 1, 1, 0)], (6, 0): [("S", 1, 1, 1), ("S", 1, 1, 2)], (7, 0): [("M", 1, 1)]}
-T1 = [[0, 1], [2], [3], [4], [5], [6, 7]]
+WARM0 = 6
+HEAD = [('W', 0, 6), ('W', 0, 1), ('U', 0, 'a', 0), ('U', 0, 'a', 1), ('W', 0, 0), ('W', 0, 5), ('W', 0, 2), ('W', 1, 0), ('U', 0, 'a', 2), ('Q', 0, 'a', 1, 1), ('U', 0, 'b', 0), ('W', 0, 3), ('Q', 0, 'b', 0, 1), ('Q', 0, 'a', 0, 1), ('U', 0, 'a', 3), ('Q', 0, 'a', 2, 1), ('T', 0, 'b', 1), ('Q', 0, 'a', 3, 1), ('W', 0, 4), ('Q', 0, 'b', 1, 1), ('C', 1)]
+PLAN = {1: [('T', 0, 'b', 2), ('T', 1, 'a', 0)], 3: [('C', 3), ('W', 0, 7), ('Q', 0, 'b', 2, 1)], 6: [('D', 1)], 7: [('T', 0, 'b', 3), ('T', 1, 'a', 3), ('W', 1, 2), ('C', 5)], 8: [('W', 1, 6), ('T', 1, 'b', 0), ('Q', 0, 'b', 3, 1), ('C', 4), ('C', 7), ('D', 2)], 9: [('T', 1, 'a', 1)], 10: [('H', 0, 0)], 11: [('H', 0, 3), ('T', 1, 'b', 1), ('G',)], 14: [('T', 1, 'b', 2), ('H', 0, 1), ('T', 1, 'a', 2)], 15: [('Q', 1, 'a', 0), ('S', 0, 0, 8, 0), ('J', 1), ('S', 0, 0, 8, 1), ('S', 0, 0, 8, 2), ('Q', 1, 'a', 1), ('H', 0, 2), ('Q', 1, 'a', 3), ('T', 1, 'b', 3), ('Q', 1, 'b', 0, 2), ('K', 0), ('Q', 1, 'a', 2), ('H', 1, 3), ('M', 0, 1), ('J', 0), ('M', 0, 0), ('Q', 1, 'b', 2, 2), ('H', 1, 2)]}
+MAIN = {(0, 1): [('H', 1, 1), ('H', 1, 0)], (0, 2): [('J', 2), ('J', 3)], (2, 0): [('L',), ('S', 1, 0, 4, 0)], (2, 3): [('S', 1, 0, 4, 1), ('S', 1, 0, 4, 2), ('K', 1)], (4, 3): [('S', 1, 4, 8, 0)], (5, 0): [('M', 1, 0)], (5, 3): [('S', 1, 4, 8, 1), ('S', 1, 4, 8, 2)], (7, 1): [('M', 1, 1)]}
+T1 = [[0, 1], [2, 3], [4], [5, 6], [7], []]
 
 
 def tile_mutualfiltercosttokenencoder_kernel(tc, fa, fb_bytes, fb_scale, g, wt, wr, out):
@@ -66,10 +51,13 @@ def tile_mutualfiltercosttokenencoder_kernel(tc, fa, fb_bytes, fb_scale, g, wt, 
         graw = kt([P, 256], BF16, "graw")
         gperm = kt([P, 2, 128], F32, "gperm")
         gcol = kt([P, NT], F32, "gcol")
+        zero = kt([P, 512], BF16, "zero")
         dummy = kt([P, 1], F32, "dummy")
         fb_raw = [kt([P, 8, 512], U8, f"fb_raw{b}") for b in range(B)]
         fb_w = [kt([P, 8, 512], BF16, f"fb_w{b}") for b in range(B)]
         fa_raw = [kt([P, 8, 512], BF16, f"fa_raw{b}") for b in range(B)]
+        fa_g = [kt([P, 4096], BF16, f"fa_g{b}") for b in range(B)]
+        fb_g = [kt([P, 4096], BF16, f"fb_g{b}") for b in range(B)]
         fa_q = [kt([P, N], U32, f"fa_q{b}") for b in range(B)]
         fa_s = [kt([P, N], U8, f"fa_s{b}") for b in range(B)]
         fb_q = [kt([P, M], U32, f"fb_q{b}") for b in range(B)]
@@ -82,7 +70,7 @@ def tile_mutualfiltercosttokenencoder_kernel(tc, fa, fb_bytes, fb_scale, g, wt, 
         wr_g = kt([P, E, 4], BF16, "wr_g")
         wr_q = kt([P, E], U32, "wr_q")
         wr_s = kt([P, E], U8, "wr_s")
-        tmax = [kt([P, 2, NT], F32, f"tmax{b}") for b in range(B)]
+        tmax = [kt([P, NT, 2], F32, f"tmax{b}") for b in range(B)]
         srow = [kt([P, 3, NT], F32, f"srow{b}") for b in range(B)]
         smap = [kt([P, M], F32, f"smap{b}") for b in range(B)]
 
@@ -99,6 +87,7 @@ def tile_mutualfiltercosttokenencoder_kernel(tc, fa, fb_bytes, fb_scale, g, wt, 
         def load_fa(b, i0, i1):
             nc.sync.dma_start(out=fa_raw[b][:, i0:i1, :], in_=fav[b][:, i0:i1, :])
 
+        nc.vector.memset(zero[:], 0.0)
         nc.sync.dma_start(out=sc4[:], in_=fb_scale.rearrange("o b (p j) -> p (o b j)", j=4))
         load_fb(0, 0)
         load_fb(0, 1)
@@ -115,6 +104,12 @@ def tile_mutualfiltercosttokenencoder_kernel(tc, fa, fb_bytes, fb_scale, g, wt, 
         nc.sync.dma_start(out=wr_raw[:], in_=wr.rearrange("(p t) e -> p t e", t=4))
         nc.sync.dma_start(out=wt_raw[:], in_=wt.rearrange("(g p t) e -> p g t e", g=2, t=4))
 
+        def warm(n):
+            bank = xbank()
+            for k in range(n):
+                nc.tensor.matmul(out=bank[:], lhsT=zero[:, 0:128], rhs=zero[:], start=True, stop=True)
+
+        warm(WARM0)
         scp = xbank()
         for j in range(4):
             nc.tensor.transpose(scp[:, 128 * j : 128 * j + 128], sc4[:, j : j + 1].to_broadcast([P, P]), ident[:])
@@ -138,43 +133,42 @@ def tile_mutualfiltercosttokenencoder_kernel(tc, fa, fb_bytes, fb_scale, g, wt, 
                 for du in range(2):
                     nc.tensor.transpose(bank[:, (2 * r + du) * 128 : (2 * r + du + 1) * 128], words[:, du::2], ident[:])
 
-        def turn_copy(which, bank):
-            grp = wk([P, 1024], BF16, "grp", bufs=8)
+        def turn_copy(which, bank, grp):
             if which == "a":
                 nc.scalar.copy(
-                    out=grp[:].bitcast(F32).rearrange("d (i r u) -> d i r u", i=2, u=2),
+                    out=grp.bitcast(F32).rearrange("d (i r u) -> d i r u", i=2, u=2),
                     in_=bank[:].rearrange("d (i u r) -> d i r u", i=2, u=2),
                 )
             else:
                 nc.scalar.copy(
-                    out=grp[:].bitcast(F32).rearrange("d (r e u) -> d r e u", e=2, u=2),
+                    out=grp.bitcast(F32).rearrange("d (r e u) -> d r e u", e=2, u=2),
                     in_=bank[:].rearrange("d (e u r) -> d r e u", e=2, u=2),
                 )
-            return grp
 
-        def turn_quant(b, which, q, grp):
+        def turn_quant(b, which, q, grp, n):
             dst, sca = (fa_q[b], fa_s[b]) if which == "a" else (fb_q[b], fb_s[b])
-            cols = slice(256 * q, 256 * q + 256)
-            nc.vector.quantize_mx(out=dst[:, cols].bitcast(FP8X4), scales=sca[:, cols], in_=grp[:])
+            cols = slice(256 * q, 256 * (q + n))
+            nc.vector.quantize_mx(out=dst[:, cols].bitcast(FP8X4), scales=sca[:, cols], in_=grp[:, 1024 * q : 1024 * (q + n)])
 
-        grps = {}
+        def grp_of(b, which):
+            return fa_g[b] if which == "a" else fb_g[b]
 
         def do_turn(b, which, q, bank):
             turn(b, which, q, bank)
-            grps[(b, which, q)] = turn_copy(which, bank)
+            turn_copy(which, bank, grp_of(b, which)[:, 1024 * q : 1024 * q + 1024])
 
-        def do_quant(b, which, q):
-            turn_quant(b, which, q, grps[(b, which, q)])
+        def do_quant(b, which, q, n=1):
+            turn_quant(b, which, q, grp_of(b, which), n)
 
         def make_gcol():
             gps = xbank()
             for u in range(2):
                 nc.tensor.transpose(gps[:, 128 * u : 128 * u + 128], gperm[:, u, :], ident[:])
             for u in range(2):
-                nc.vector.tensor_scalar(
+                nc.scalar.activation(
                     out=gcol[:].rearrange("q (g u h) -> q u g h", g=2, u=2)[:, u],
-                    in0=gps[:, 128 * u : 128 * u + 4].rearrange("q (g h) -> q g h", g=2),
-                    scalar1=float(D) ** -0.5, scalar2=None, op0=ALU.mult,
+                    in_=gps[:, 128 * u : 128 * u + 4].rearrange("q (g h) -> q g h", g=2),
+                    func=ACT.Copy, scale=float(D) ** -0.5,
                 )
 
         def mm_c(b, lq, ls, rq, rs, i, h, bank):
@@ -194,17 +188,16 @@ def tile_mutualfiltercosttokenencoder_kernel(tc, fa, fb_bytes, fb_scale, g, wt, 
             mm_c(b, fa_q, fa_s, fb_q, fb_s, i, h, bank)
 
         def rd_t(b, i, h, bank):
-            nc.vector.reduce_max(out=tmax[b][:, h, i : i + 1], in_=bank[:], axis=X)
+            nc.vector.reduce_max(out=tmax[b][:, i, h : h + 1], in_=bank[:], axis=X)
 
-        def s_cols(b, half, step):
-            cols = slice(4 * half, 4 * half + 4)
+        def s_cols(b, i0, i1, step):
             if step == 0:
-                nc.vector.reduce_max(out=srow[b][:, 0, cols], in_=tmax[b][:, :, cols].rearrange("q h i -> q i h"), axis=X)
+                nc.vector.reduce_max(out=srow[b][:, 0, i0:i1], in_=tmax[b][:, i0:i1, :], axis=X)
             elif step == 1:
-                nc.vector.reciprocal(out=srow[b][:, 1, cols], in_=srow[b][:, 0, cols])
+                nc.vector.reciprocal(out=srow[b][:, 1, i0:i1], in_=srow[b][:, 0, i0:i1])
             else:
                 eng = nc.vector if b == 0 else nc.gpsimd
-                eng.tensor_tensor(out=srow[b][:, 2, cols], in0=srow[b][:, 1, cols], in1=gcol[:, cols], op=ALU.mult)
+                eng.tensor_tensor(out=srow[b][:, 2, i0:i1], in0=srow[b][:, 1, i0:i1], in1=gcol[:, i0:i1], op=ALU.mult)
 
         def s_map(b, half):
             bank = xbank()
@@ -218,7 +211,7 @@ def tile_mutualfiltercosttokenencoder_kernel(tc, fa, fb_bytes, fb_scale, g, wt, 
             out=gperm[:].rearrange("r u (q e) -> r u q e", e=2), in0=graw[:].rearrange("r (q u e) -> r u q e", u=2, e=2),
             scalar1=1.0, scalar2=1.0, op0=ALU.mult, op1=ALU.mult,
         )
-        order = [(i, h) for i in range(NT) for h in range(2)]
+        order = [(0, 0), (1, 0), (0, 1), (1, 1)] + [(i, h) for i in range(2, NT) for h in range(2)]
         tb = {}
         casts = {}
 
@@ -244,14 +237,15 @@ def tile_mutualfiltercosttokenencoder_kernel(tc, fa, fb_bytes, fb_scale, g, wt, 
             cols = slice(128 * k, 128 * k + 128)
             nc.scalar.copy(out=wr_g[:, cols], in_=wr_raw[:, :, cols].rearrange("p t e -> p e t"))
 
-        def wt_s_i(k):
+        def wt_s_i(t, k):
             cols = slice(128 * k, 128 * k + 128)
-            nc.scalar.copy(out=wt_g[:, 1, cols], in_=wt_raw[:, 1, :, cols].rearrange("p t e -> p e t"))
+            nc.scalar.copy(out=wt_g[:, t, cols], in_=wt_raw[:, t, :, cols].rearrange("p t e -> p e t"))
 
         def wr_quant():
             nc.vector.quantize_mx(out=wr_q[:].bitcast(FP8X4), scales=wr_s[:], in_=wr_g[:].rearrange("p e t -> p (e t)"))
 
         ops = dict(
+            D=warm,
             T=lambda b, w, q: do_turn(b, w, q, xbank()), U=lambda b, w, q: do_turn(b, w, q, cbank()), Q=do_quant, W=widen_v, C=cast_g, G=make_gcol,
             S=s_cols, M=s_map, I=wt_i, J=wr_i, H=wt_s_i, K=wt_quant, L=wr_quant,
         )
@@ -296,42 +290,53 @@ def tile_mutualfiltercosttokenencoder_kernel(tc, fa, fb_bytes, fb_scale, g, wt, 
 
         def turn_f(s, part):
             if part == 0:
-                words = fgt[s][:].bitcast(F32)
                 fbk[s] = xbank()
-                for k in range(4):
-                    nc.tensor.transpose(fbk[s][:, 128 * k : 128 * k + 128], words[:, 128 * k : 128 * k + 128], ident[:])
+                turn_words(s, 0, 4)
             else:
                 grpf[s] = wk([P, 1024], BF16, "grpf")
-                nc.scalar.copy(
-                    out=grpf[s][:].bitcast(F32).rearrange("p (g n u) -> p g n u", g=2, u=2),
-                    in_=fbk[s][:].rearrange("p (g u n) -> p g n u", g=2, u=2),
-                )
+                turn_out(nc.scalar.copy, s, 0, 2)
+
+        def turn_words(s, k0, k1):
+            words = fgt[s][:].bitcast(F32)
+            for k in range(k0, k1):
+                nc.tensor.transpose(fbk[s][:, 128 * k : 128 * k + 128], words[:, 128 * k : 128 * k + 128], ident[:])
+
+        def turn_out(copy, s, g0, g1):
+            copy(
+                out=grpf[s][:, 512 * g0 : 512 * g1].bitcast(F32).rearrange("p (g n u) -> p g n u", g=g1 - g0, u=2),
+                in_=fbk[s][:, 256 * g0 : 256 * g1].rearrange("p (g u n) -> p g n u", g=g1 - g0, u=2),
+            )
 
         fqs = {}
 
-        def quant_f(s):
-            fq = wk([P, 256], U32, "fq")
-            fs = wk([P, 256], U8, "fs")
-            nc.vector.quantize_mx(out=fq[:].bitcast(FP8X4), scales=fs[:], in_=grpf[s][:])
-            fqs[s] = (fq, fs)
+        def quant_f(s, g0=0, g1=2):
+            if g0 == 0:
+                fqs[s] = (wk([P, 256], U32, "fq"), wk([P, 256], U8, "fs"))
+            fq, fs = fqs[s]
+            cols = slice(128 * g0, 128 * g1)
+            nc.vector.quantize_mx(out=fq[:, cols].bitcast(FP8X4), scales=fs[:, cols], in_=grpf[s][:, 512 * g0 : 512 * g1])
 
         obs = {}
 
-        def mm_out(s):
-            b2, i2 = s // NT, s % NT
-            fq, fs = fqs[s]
-            o = xbank()
-            rows = slice(128 * i2, 128 * i2 + 128)
+        def mm_out_r(s, o):
+            rows = slice(128 * (s % NT), 128 * (s % NT) + 128)
             nc.tensor.matmul_mx(
-                out=o[:], lhsT=fa_q[b2][:, rows].bitcast(FP8X4), lhsT_scale=fa_s[b2][:, rows],
+                out=o[:], lhsT=fa_q[s // NT][:, rows].bitcast(FP8X4), lhsT_scale=fa_s[s // NT][:, rows],
                 rhs=wr_q[:].bitcast(FP8X4), rhs_scale=wr_s[:], start=True, stop=False,
             )
+            obs[s] = o
+
+        def mm_out_t(s):
+            fq, fs = fqs[s]
             for t in range(2):
                 nc.tensor.matmul_mx(
-                    out=o[:], lhsT=fq[:, 128 * t : 128 * t + 128].bitcast(FP8X4), lhsT_scale=fs[:, 128 * t : 128 * t + 128],
+                    out=obs[s][:], lhsT=fq[:, 128 * t : 128 * t + 128].bitcast(FP8X4), lhsT_scale=fs[:, 128 * t : 128 * t + 128],
                     rhs=wt_q[:, t].bitcast(FP8X4), rhs_scale=wt_s[:, t], start=False, stop=(t == 1),
                 )
-            obs[s] = o
+
+        def mm_out(s):
+            mm_out_r(s, xbank())
+            mm_out_t(s)
 
         def store(s):
             ot = wk([P, E], F32, "ot", bufs=4)
@@ -340,7 +345,7 @@ def tile_mutualfiltercosttokenencoder_kernel(tc, fa, fb_bytes, fb_scale, g, wt, 
 
         issue_n(0, 0)
         issue_n(0, 1)
-        for s in range(STEPS + 3):
+        for s in range(STEPS):
             live, prv = s < STEPS, 1 <= s <= STEPS
             tq = [(it, h) for it in (T1[s] if s < len(T1) else []) for h in range(2)]
             tbk = {}
@@ -369,14 +374,16 @@ def tile_mutualfiltercosttokenencoder_kernel(tc, fa, fb_bytes, fb_scale, g, wt, 
                 weigh(s, 0)
             if 2 <= s <= STEPS + 1:
                 turn_f(s - 2, 0)
+            if prv:
+                nc.vector.reciprocal(out=arc[s - 1][:, 1:2], in_=arc[s - 1][:, 0:1])
             extra(0)
             t_mm(1)
             if live:
                 row_max(s, 1)
                 square(s, 1)
-                weigh(s, 1)
+                if s < STEPS - 1:
+                    weigh(s, 1)
             if prv:
-                nc.vector.reciprocal(out=arc[s - 1][:, 1:2], in_=arc[s - 1][:, 0:1])
                 fgt[s - 1] = wk([P, M], BF16, "fg")
             if 2 <= s <= STEPS + 1:
                 turn_f(s - 2, 1)
@@ -399,3 +406,35 @@ def tile_mutualfiltercosttokenencoder_kernel(tc, fa, fb_bytes, fb_scale, g, wt, 
                 t_mm(k)
                 t_rd(k)
             extra(3)
+
+        last = STEPS - 1
+        turn_f(last - 1, 0)
+        for s in (last - 2, last - 1):
+            mm_out_r(s, cbank())
+        nc.vector.tensor_tensor(out=sq[last][:, 512:1024], in0=sq[last][:, 512:1024], in1=smap[1][:, 512:1024], op=ALU.mult)
+        turn_f(last - 1, 1)
+        nc.vector.reciprocal(out=arc[last][:, 1:2], in_=arc[last][:, 0:1])
+        quant_f(last - 2)
+        mm_out_t(last - 2)
+        fgt[last] = wk([P, M], BF16, "fg")
+        product(last, 0)
+        fbk[last] = xbank()
+        grpf[last] = wk([P, 1024], BF16, "grpf")
+        turn_words(last, 0, 2)
+        store(last - 2)
+        product(last, 1)
+        turn_words(last, 2, 4)
+        turn_out(nc.scalar.copy, last, 0, 1)
+        quant_f(last - 1)
+        turn_out(nc.vector.tensor_copy, last, 1, 2)
+        mm_out_r(last, cbank())
+        mm_out_t(last - 1)
+        quant_f(last, 0, 1)
+        quant_f(last, 1, 2)
+        mm_out_t(last)
+        store(last - 1)
+        orow = out[1].rearrange("(p i) e -> p i e", i=8)[:, 7, :]
+        for h, copy in ((0, nc.vector.tensor_copy), (1, nc.scalar.copy)):
+            half = wk([P, 256], F32, "half", bufs=2)
+            copy(out=half[:], in_=obs[last][:, 256 * h : 256 * h + 256])
+            nc.sync.dma_start(out=orow[:, 256 * h : 256 * h + 256], in_=half[:])

from contextlib import ExitStack

import concourse.mybir as mybir
from concourse.masks import make_identity

F32 = mybir.dt.float32
BF16 = mybir.dt.bfloat16
U32 = mybir.dt.uint32
U8 = mybir.dt.uint8
FP8 = mybir.dt.float8_e4m3fn
FP8X4 = mybir.dt.float8_e4m3fn_x4
ALU = mybir.AluOpType
ACT = mybir.ActivationFunctionType
X = mybir.AxisListType.X

B, N, M, D, E = 2, 1024, 1024, 512, 512
P = 128
NT = N // P
FLOPS = 2 * B * N * M * D + 2 * B * N * M * E + 2 * B * N * D * E

WARM0 = 6
HEAD = [('W', 0, 6), ('W', 0, 1), ('U', 0, 'a', 0), ('U', 0, 'a', 1), ('W', 0, 0), ('W', 0, 5), ('W', 0, 2), ('W', 1, 0), ('U', 0, 'a', 2), ('Q', 0, 'a', 1, 1), ('U', 0, 'b', 0), ('W', 0, 3), ('Q', 0, 'b', 0, 1), ('Q', 0, 'a', 0, 1), ('U', 0, 'a', 3), ('Q', 0, 'a', 2, 1), ('T', 0, 'b', 1), ('Q', 0, 'a', 3, 1), ('W', 0, 4), ('Q', 0, 'b', 1, 1), ('C', 1)]
PLAN = {1: [('T', 0, 'b', 2), ('T', 1, 'a', 0)], 3: [('C', 3), ('W', 0, 7), ('Q', 0, 'b', 2, 1)], 6: [('D', 1)], 7: [('T', 0, 'b', 3), ('T', 1, 'a', 3), ('W', 1, 2), ('C', 5)], 8: [('W', 1, 6), ('T', 1, 'b', 0), ('Q', 0, 'b', 3, 1), ('C', 4), ('C', 7), ('D', 2)], 9: [('T', 1, 'a', 1)], 10: [('H', 0, 0)], 11: [('H', 0, 3), ('T', 1, 'b', 1), ('G',)], 14: [('T', 1, 'b', 2), ('H', 0, 1), ('T', 1, 'a', 2)], 15: [('Q', 1, 'a', 0), ('S', 0, 0, 8, 0), ('J', 1), ('S', 0, 0, 8, 1), ('S', 0, 0, 8, 2), ('Q', 1, 'a', 1), ('H', 0, 2), ('Q', 1, 'a', 3), ('T', 1, 'b', 3), ('Q', 1, 'b', 0, 2), ('K', 0), ('Q', 1, 'a', 2), ('H', 1, 3), ('M', 0, 1), ('J', 0), ('M', 0, 0), ('Q', 1, 'b', 2, 2), ('H', 1, 2)]}
MAIN = {(0, 1): [('H', 1, 1), ('H', 1, 0)], (0, 2): [('J', 2), ('J', 3)], (2, 0): [('L',), ('S', 1, 0, 4, 0)], (2, 3): [('S', 1, 0, 4, 1), ('S', 1, 0, 4, 2), ('K', 1)], (4, 3): [('S', 1, 4, 8, 0)], (5, 0): [('M', 1, 0)], (5, 3): [('S', 1, 4, 8, 1), ('S', 1, 4, 8, 2)], (7, 1): [('M', 1, 1)]}
T1 = [[0, 1], [2, 3], [4], [5, 6], [7], []]


def tile_mutualfiltercosttokenencoder_kernel(tc, fa, fb_bytes, fb_scale, g, wt, wr, out):
    nc = tc.nc
    with ExitStack() as ctx:
        keep = ctx.enter_context(tc.tile_pool(name="keep", bufs=1))
        work = ctx.enter_context(tc.tile_pool(name="work", bufs=3))
        cps = ctx.enter_context(tc.psum_pool(name="cps", bufs=5))
        xps = ctx.enter_context(tc.psum_pool(name="xps", bufs=3))

        def kt(shape, dt, nm):
            return keep.tile(shape, dt, name=nm, tag=nm, align_bytes=64)

        def wk(shape, dt, nm, bufs=3):
            return work.tile(shape, dt, name=nm, tag=nm, bufs=bufs, align_bytes=64)

        def cbank():
            return cps.tile([P, 512], F32, name="cbank", tag="c")

        def xbank():
            return xps.tile([P, 512], F32, name="xbank", tag="x")

        ident = kt([P, P], F32, "ident")
        sc4 = kt([P, 4], F32, "sc4")
        scb = kt([P, 512], F32, "scb")
        graw = kt([P, 256], BF16, "graw")
        gperm = kt([P, 2, 128], F32, "gperm")
        gcol = kt([P, NT], F32, "gcol")
        zero = kt([P, 512], BF16, "zero")
        dummy = kt([P, 1], F32, "dummy")
        fb_raw = [kt([P, 8, 512], U8, f"fb_raw{b}") for b in range(B)]
        fb_w = [kt([P, 8, 512], BF16, f"fb_w{b}") for b in range(B)]
        fa_raw = [kt([P, 8, 512], BF16, f"fa_raw{b}") for b in range(B)]
        fa_g = [kt([P, 4096], BF16, f"fa_g{b}") for b in range(B)]
        fb_g = [kt([P, 4096], BF16, f"fb_g{b}") for b in range(B)]
        fa_q = [kt([P, N], U32, f"fa_q{b}") for b in range(B)]
        fa_s = [kt([P, N], U8, f"fa_s{b}") for b in range(B)]
        fb_q = [kt([P, M], U32, f"fb_q{b}") for b in range(B)]
        fb_s = [kt([P, M], U8, f"fb_s{b}") for b in range(B)]
        wt_raw = kt([P, 2, 4, E], BF16, "wt_raw")
        wt_g = kt([P, 2, E, 4], BF16, "wt_g")
        wt_q = kt([P, 2, E], U32, "wt_q")
        wt_s = kt([P, 2, E], U8, "wt_s")
        wr_raw = kt([P, 4, E], BF16, "wr_raw")
        wr_g = kt([P, E, 4], BF16, "wr_g")
        wr_q = kt([P, E], U32, "wr_q")
        wr_s = kt([P, E], U8, "wr_s")
        tmax = [kt([P, NT, 2], F32, f"tmax{b}") for b in range(B)]
        srow = [kt([P, 3, NT], F32, f"srow{b}") for b in range(B)]
        smap = [kt([P, M], F32, f"smap{b}") for b in range(B)]

        ctx.enter_context(tc.manual_schedule())

        fbv = [fb_bytes[b].rearrange("(g p j) d -> p g j d", g=2, j=4) for b in range(B)]
        fav = [fa[b].rearrange("(p i) d -> p i d", i=8) for b in range(B)]

        nc.gpsimd.memset(graw[:], 0.0)

        def load_fb(b, gg):
            nc.sync.dma_start(out=fb_raw[b][:, 4 * gg : 4 * gg + 4, :], in_=fbv[b][:, gg])

        def load_fa(b, i0, i1):
            nc.sync.dma_start(out=fa_raw[b][:, i0:i1, :], in_=fav[b][:, i0:i1, :])

        nc.vector.memset(zero[:], 0.0)
        nc.sync.dma_start(out=sc4[:], in_=fb_scale.rearrange("o b (p j) -> p (o b j)", j=4))
        load_fb(0, 0)
        load_fb(0, 1)
        nc.sync.dma_start(out=graw[0:4, :], in_=g.rearrange("(r f) -> r f", r=4))
        for q in range(4):
            load_fa(0, 2 * q, 2 * q + 2)
        make_identity(nc, ident[:])
        nc.vector.memset(dummy[:], 0.0)
        nc.scalar.activation(out=dummy[:], in_=dummy[:], func=ACT.Square)
        load_fb(1, 0)
        load_fb(1, 1)
        load_fa(1, 0, 4)
        load_fa(1, 4, 8)
        nc.sync.dma_start(out=wr_raw[:], in_=wr.rearrange("(p t) e -> p t e", t=4))
        nc.sync.dma_start(out=wt_raw[:], in_=wt.rearrange("(g p t) e -> p g t e", g=2, t=4))

        def warm(n):
            bank = xbank()
            for k in range(n):
                nc.tensor.matmul(out=bank[:], lhsT=zero[:, 0:128], rhs=zero[:], start=True, stop=True)

        warm(WARM0)
        scp = xbank()
        for j in range(4):
            nc.tensor.transpose(scp[:, 128 * j : 128 * j + 128], sc4[:, j : j + 1].to_broadcast([P, P]), ident[:])
        nc.scalar.copy(out=scb[:].rearrange("q (p j) -> q p j", j=4), in_=scp[:].rearrange("q (j p) -> q p j", j=4))

        def widen_v(b, gj):
            nc.vector.tensor_tensor(out=fb_w[b][:, gj, :], in0=fb_raw[b][:, gj, :].bitcast(FP8), in1=scb[:], op=ALU.mult)

        def widen_s(b, gj):
            cast = wk([P, 512], BF16, "cast", bufs=4)
            nc.scalar.copy(out=cast[:], in_=fb_raw[b][:, gj, :].bitcast(FP8))
            return cast

        def widen_g(b, gj, cast):
            nc.gpsimd.tensor_tensor(out=fb_w[b][:, gj, :], in0=cast[:], in1=scb[:], op=ALU.mult)

        def turn(b, which, q, bank):
            src = fa_raw[b] if which == "a" else fb_w[b]
            for r in range(2):
                words = src[:, 2 * q + r, :].bitcast(F32)
                for du in range(2):
                    nc.tensor.transpose(bank[:, (2 * r + du) * 128 : (2 * r + du + 1) * 128], words[:, du::2], ident[:])

        def turn_copy(which, bank, grp):
            if which == "a":
                nc.scalar.copy(
                    out=grp.bitcast(F32).rearrange("d (i r u) -> d i r u", i=2, u=2),
                    in_=bank[:].rearrange("d (i u r) -> d i r u", i=2, u=2),
                )
            else:
                nc.scalar.copy(
                    out=grp.bitcast(F32).rearrange("d (r e u) -> d r e u", e=2, u=2),
                    in_=bank[:].rearrange("d (e u r) -> d r e u", e=2, u=2),
                )

        def turn_quant(b, which, q, grp, n):
            dst, sca = (fa_q[b], fa_s[b]) if which == "a" else (fb_q[b], fb_s[b])
            cols = slice(256 * q, 256 * (q + n))
            nc.vector.quantize_mx(out=dst[:, cols].bitcast(FP8X4), scales=sca[:, cols], in_=grp[:, 1024 * q : 1024 * (q + n)])

        def grp_of(b, which):
            return fa_g[b] if which == "a" else fb_g[b]

        def do_turn(b, which, q, bank):
            turn(b, which, q, bank)
            turn_copy(which, bank, grp_of(b, which)[:, 1024 * q : 1024 * q + 1024])

        def do_quant(b, which, q, n=1):
            turn_quant(b, which, q, grp_of(b, which), n)

        def make_gcol():
            gps = xbank()
            for u in range(2):
                nc.tensor.transpose(gps[:, 128 * u : 128 * u + 128], gperm[:, u, :], ident[:])
            for u in range(2):
                nc.scalar.activation(
                    out=gcol[:].rearrange("q (g u h) -> q u g h", g=2, u=2)[:, u],
                    in_=gps[:, 128 * u : 128 * u + 4].rearrange("q (g h) -> q g h", g=2),
                    func=ACT.Copy, scale=float(D) ** -0.5,
                )

        def mm_c(b, lq, ls, rq, rs, i, h, bank):
            nc.tensor.matmul_mx(
                out=bank[:],
                lhsT=lq[b][:, 128 * i : 128 * i + 128].bitcast(FP8X4),
                lhsT_scale=ls[b][:, 128 * i : 128 * i + 128],
                rhs=rq[b][:, 512 * h : 512 * h + 512].bitcast(FP8X4),
                rhs_scale=rs[b][:, 512 * h : 512 * h + 512],
                start=True, stop=True,
            )

        def mm_t(b, i, h, bank):
            mm_c(b, fb_q, fb_s, fa_q, fa_s, i, h, bank)

        def mm_n(b, i, h, bank):
            mm_c(b, fa_q, fa_s, fb_q, fb_s, i, h, bank)

        def rd_t(b, i, h, bank):
            nc.vector.reduce_max(out=tmax[b][:, i, h : h + 1], in_=bank[:], axis=X)

        def s_cols(b, i0, i1, step):
            if step == 0:
                nc.vector.reduce_max(out=srow[b][:, 0, i0:i1], in_=tmax[b][:, i0:i1, :], axis=X)
            elif step == 1:
                nc.vector.reciprocal(out=srow[b][:, 1, i0:i1], in_=srow[b][:, 0, i0:i1])
            else:
                eng = nc.vector if b == 0 else nc.gpsimd
                eng.tensor_tensor(out=srow[b][:, 2, i0:i1], in0=srow[b][:, 1, i0:i1], in1=gcol[:, i0:i1], op=ALU.mult)

        def s_map(b, half):
            bank = xbank()
            for k in range(4):
                i = 4 * half + k
                nc.tensor.transpose(bank[:, 128 * k : 128 * k + 128], srow[b][:, 2, i : i + 1].to_broadcast([P, P]), ident[:])
            nc.scalar.copy(out=smap[b][:, 512 * half : 512 * half + 512], in_=bank[:])


        nc.gpsimd.tensor_scalar(
            out=gperm[:].rearrange("r u (q e) -> r u q e", e=2), in0=graw[:].rearrange("r (q u e) -> r u q e", u=2, e=2),
            scalar1=1.0, scalar2=1.0, op0=ALU.mult, op1=ALU.mult,
        )
        order = [(0, 0), (1, 0), (0, 1), (1, 1)] + [(i, h) for i in range(2, NT) for h in range(2)]
        tb = {}
        casts = {}

        def issue_t0(k):
            if k < 16:
                tb[k] = cbank()
                mm_t(0, order[k][0], order[k][1], tb[k])

        def cast_g(gj):
            casts[gj] = widen_s(1, gj)
            widen_g(1, gj, casts[gj])

        def wt_i(t):
            nc.gpsimd.tensor_scalar(
                out=wt_g[:, t], in0=wt_raw[:, t].rearrange("p t e -> p e t"),
                scalar1=1.0, scalar2=1.0, op0=ALU.mult, op1=ALU.mult,
            )

        def wt_quant(t):
            nc.vector.quantize_mx(out=wt_q[:, t].bitcast(FP8X4), scales=wt_s[:, t], in_=wt_g[:, t].rearrange("p e t -> p (e t)"))

        def wr_i(k):
            cols = slice(128 * k, 128 * k + 128)
            nc.scalar.copy(out=wr_g[:, cols], in_=wr_raw[:, :, cols].rearrange("p t e -> p e t"))

        def wt_s_i(t, k):
            cols = slice(128 * k, 128 * k + 128)
            nc.scalar.copy(out=wt_g[:, t, cols], in_=wt_raw[:, t, :, cols].rearrange("p t e -> p e t"))

        def wr_quant():
            nc.vector.quantize_mx(out=wr_q[:].bitcast(FP8X4), scales=wr_s[:], in_=wr_g[:].rearrange("p e t -> p (e t)"))

        ops = dict(
            D=warm,
            T=lambda b, w, q: do_turn(b, w, q, xbank()), U=lambda b, w, q: do_turn(b, w, q, cbank()), Q=do_quant, W=widen_v, C=cast_g, G=make_gcol,
            S=s_cols, M=s_map, I=wt_i, J=wr_i, H=wt_s_i, K=wt_quant, L=wr_quant,
        )
        for o in HEAD:
            ops[o[0]](*o[1:])

        for k in range(4):
            issue_t0(k)
        for k in range(16):
            rd_t(0, order[k][0], order[k][1], tb[k])
            for o in PLAN.get(k, []):
                ops[o[0]](*o[1:])
            issue_t0(k + 4)

        STEPS = 2 * NT
        nb, sq, fgt, amx, arc, grpf = {}, {}, {}, {}, {}, {}

        def issue_n(s, h):
            if s < STEPS:
                nb[(s, h)] = cbank()
                mm_n(s // NT, s % NT, h, nb[(s, h)])

        def row_max(s, h):
            nc.vector.reduce_max(out=amx[s][:, h : h + 1], in_=nb[(s, h)][:], axis=X)

        def square(s, h):
            cols = slice(512 * h, 512 * h + 512)
            nc.scalar.activation(out=sq[s][:, cols], in_=nb[(s, h)][:], func=ACT.Square)

        def weigh(s, h):
            cols = slice(512 * h, 512 * h + 512)
            nc.gpsimd.tensor_tensor(out=sq[s][:, cols], in0=sq[s][:, cols], in1=smap[s // NT][:, cols], op=ALU.mult)

        def product(s, h):
            cols = slice(512 * h, 512 * h + 512)
            nc.vector.scalar_tensor_tensor(
                out=fgt[s][:, cols], in0=nb[(s, h)][:], scalar=arc[s][:, 1:2], in1=sq[s][:, cols],
                op0=ALU.mult, op1=ALU.mult,
            )

        fbk = {}

        def turn_f(s, part):
            if part == 0:
                fbk[s] = xbank()
                turn_words(s, 0, 4)
            else:
                grpf[s] = wk([P, 1024], BF16, "grpf")
                turn_out(nc.scalar.copy, s, 0, 2)

        def turn_words(s, k0, k1):
            words = fgt[s][:].bitcast(F32)
            for k in range(k0, k1):
                nc.tensor.transpose(fbk[s][:, 128 * k : 128 * k + 128], words[:, 128 * k : 128 * k + 128], ident[:])

        def turn_out(copy, s, g0, g1):
            copy(
                out=grpf[s][:, 512 * g0 : 512 * g1].bitcast(F32).rearrange("p (g n u) -> p g n u", g=g1 - g0, u=2),
                in_=fbk[s][:, 256 * g0 : 256 * g1].rearrange("p (g u n) -> p g n u", g=g1 - g0, u=2),
            )

        fqs = {}

        def quant_f(s, g0=0, g1=2):
            if g0 == 0:
                fqs[s] = (wk([P, 256], U32, "fq"), wk([P, 256], U8, "fs"))
            fq, fs = fqs[s]
            cols = slice(128 * g0, 128 * g1)
            nc.vector.quantize_mx(out=fq[:, cols].bitcast(FP8X4), scales=fs[:, cols], in_=grpf[s][:, 512 * g0 : 512 * g1])

        obs = {}

        def mm_out_r(s, o):
            rows = slice(128 * (s % NT), 128 * (s % NT) + 128)
            nc.tensor.matmul_mx(
                out=o[:], lhsT=fa_q[s // NT][:, rows].bitcast(FP8X4), lhsT_scale=fa_s[s // NT][:, rows],
                rhs=wr_q[:].bitcast(FP8X4), rhs_scale=wr_s[:], start=True, stop=False,
            )
            obs[s] = o

        def mm_out_t(s):
            fq, fs = fqs[s]
            for t in range(2):
                nc.tensor.matmul_mx(
                    out=obs[s][:], lhsT=fq[:, 128 * t : 128 * t + 128].bitcast(FP8X4), lhsT_scale=fs[:, 128 * t : 128 * t + 128],
                    rhs=wt_q[:, t].bitcast(FP8X4), rhs_scale=wt_s[:, t], start=False, stop=(t == 1),
                )

        def mm_out(s):
            mm_out_r(s, xbank())
            mm_out_t(s)

        def store(s):
            ot = wk([P, E], F32, "ot", bufs=4)
            nc.scalar.copy(out=ot[:], in_=obs[s][:])
            nc.sync.dma_start(out=out[s // NT].rearrange("(p i) e -> p i e", i=8)[:, s % NT, :], in_=ot[:])

        issue_n(0, 0)
        issue_n(0, 1)
        for s in range(STEPS):
            live, prv = s < STEPS, 1 <= s <= STEPS
            tq = [(it, h) for it in (T1[s] if s < len(T1) else []) for h in range(2)]
            tbk = {}

            def t_mm(k):
                if k < len(tq):
                    tbk[k] = xbank()
                    mm_t(1, tq[k][0], tq[k][1], tbk[k])

            def t_rd(k):
                if k < len(tq):
                    rd_t(1, tq[k][0], tq[k][1], tbk[k])

            def extra(pos):
                for o in MAIN.get((s, pos), []):
                    ops[o[0]](*o[1:])

            t_mm(0)
            t_rd(0)
            if live:
                amx[s] = wk([P, 2], F32, "amx", bufs=4)
                arc[s] = wk([P, 2], F32, "arc", bufs=4)
                sq[s] = wk([P, M], F32, "sq", bufs=4)
                row_max(s, 0)
                square(s, 0)
                weigh(s, 0)
            if 2 <= s <= STEPS + 1:
                turn_f(s - 2, 0)
            if prv:
                nc.vector.reciprocal(out=arc[s - 1][:, 1:2], in_=arc[s - 1][:, 0:1])
            extra(0)
            t_mm(1)
            if live:
                row_max(s, 1)
                square(s, 1)
                if s < STEPS - 1:
                    weigh(s, 1)
            if prv:
                fgt[s - 1] = wk([P, M], BF16, "fg")
            if 2 <= s <= STEPS + 1:
                turn_f(s - 2, 1)
            extra(1)
            if s >= 3:
                quant_f(s - 3)
                mm_out(s - 3)
                store(s - 3)
            if prv:
                product(s - 1, 0)
            issue_n(s + 1, 0)
            t_rd(1)
            extra(2)
            if prv:
                product(s - 1, 1)
            issue_n(s + 1, 1)
            if live:
                nc.vector.reduce_max(out=arc[s][:, 0:1], in_=amx[s][:], axis=X)
            for k in range(2, len(tq)):
                t_mm(k)
                t_rd(k)
            extra(3)

        last = STEPS - 1
        turn_f(last - 1, 0)
        for s in (last - 2, last - 1):
            mm_out_r(s, cbank())
        nc.vector.tensor_tensor(out=sq[last][:, 512:1024], in0=sq[last][:, 512:1024], in1=smap[1][:, 512:1024], op=ALU.mult)
        turn_f(last - 1, 1)
        nc.vector.reciprocal(out=arc[last][:, 1:2], in_=arc[last][:, 0:1])
        quant_f(last - 2)
        mm_out_t(last - 2)
        fgt[last] = wk([P, M], BF16, "fg")
        product(last, 0)
        fbk[last] = xbank()
        grpf[last] = wk([P, 1024], BF16, "grpf")
        turn_words(last, 0, 2)
        store(last - 2)
        product(last, 1)
        turn_words(last, 2, 4)
        turn_out(nc.scalar.copy, last, 0, 1)
        quant_f(last - 1)
        turn_out(nc.vector.tensor_copy, last, 1, 2)
        mm_out_r(last, cbank())
        mm_out_t(last - 1)
        quant_f(last, 0, 1)
        quant_f(last, 1, 2)
        mm_out_t(last)
        store(last - 1)
        orow = out[1].rearrange("(p i) e -> p i e", i=8)[:, 7, :]
        for h, copy in ((0, nc.vector.tensor_copy), (1, nc.scalar.copy)):
            half = wk([P, 256], F32, "half", bufs=2)
            copy(out=half[:], in_=obs[last][:, 256 * h : 256 * h + 256])
            nc.sync.dma_start(out=orow[:, 256 * h : 256 * h + 256], in_=half[:])
